import numpy as np
import ml_dtypes


def mxq(x, axis, fmt="e4m3"):
    dtype, down = {"e4m3": (ml_dtypes.float8_e4m3fn, 7), "e5m2": (ml_dtypes.float8_e5m2, 14)}[fmt]
    v = np.moveaxis(np.asarray(x, np.float32).astype(ml_dtypes.bfloat16).astype(np.float64), axis, -1)
    blocks = v.reshape(v.shape[:-1] + (-1, 32))
    amax = np.abs(blocks).max(-1, keepdims=True)
    byte = np.maximum(np.where(amax > 0, np.frexp(amax)[1] - 1 + 127, 0) - down, 1)
    scale = np.exp2(byte - 127.0)
    codes = (blocks / scale).astype(np.float32).astype(dtype).astype(np.float64)
    return np.moveaxis((codes * scale).reshape(v.shape), -1, axis)


WIDE = False


def mx_kscale(k):
    if not WIDE:
        return np.ones(k)
    levels = np.array([24, -24, 12, -12, 0])
    if k % 512:
        return np.exp2(np.random.permutation(np.resize(levels, k // 32))).repeat(32)
    a = np.empty((k // 512, 16))
    for p in range(k // 512):
        a[p, :8] = np.random.permutation(np.resize(levels, 8))
        for g in range(8):
            far = levels[np.abs(levels - a[p, g]) >= 10]
            a[p, g + 8] = far[np.random.randint(len(far))]
    return np.exp2(a.ravel()).repeat(32)


def f64(x):
    return np.asarray(x).astype(np.float64)


def striped(idx):
    return np.tile(idx.reshape(-1, 16).T, (8, 1)).astype(np.uint16)


def unstriped(offs):
    return offs[:16].T.reshape(-1).astype(np.int64)


E2M1 = np.array([0.0, 0.5, 1.0, 1.5, 2.0, 3.0, 4.0, 6.0, -0.0, -0.5, -1.0, -1.5, -2.0, -3.0, -4.0, -6.0])


def pack_weight(w, fmt):
    k, n = w.shape
    w = f64(np.asarray(w, np.float32).astype(ml_dtypes.bfloat16)).reshape(k // 32, 32, n)
    amax = np.abs(w).max(1)
    if fmt == "e4m3":
        byte = np.frexp(amax)[1] - 1 + 127 - 7
    else:
        mant, ex = np.frexp(amax / 6.0)
        byte = np.where(mant > 0.5, ex, ex - 1) + 127
    byte = np.clip(np.where(amax > 0, byte, 1), 1, 254)
    scaled = (w * np.exp2(127.0 - byte)[:, None, :]).reshape(k, n).astype(np.float32)
    by_word = np.ascontiguousarray(scaled.reshape(k // 512, 128, 4, n).transpose(0, 1, 3, 2))
    if fmt == "e4m3":
        words = by_word.astype(ml_dtypes.float8_e4m3fn).view(np.uint8)
    else:
        c = by_word.astype(ml_dtypes.float4_e2m1fn).view(np.uint8) & 0xF
        words = (c[..., 0::2] | (c[..., 1::2] << 4)).reshape(k // 512, 128, 2 * n)
    return np.ascontiguousarray(words), np.ascontiguousarray(byte.astype(np.uint8).reshape(k // 512, 16, n))


def unpack_weight(words, scales, fmt):
    g, _, n = scales.shape
    words = np.ascontiguousarray(words).reshape(g, 128, n, -1)
    if fmt == "e4m3":
        vals = words.view(ml_dtypes.float8_e4m3fn).astype(np.float64)
    else:
        nib = np.empty((g, 128, n, 4), np.uint8)
        nib[..., 0::2] = words & 0xF
        nib[..., 1::2] = words >> 4
        vals = E2M1[nib]
    vals = vals * np.repeat(np.exp2(scales.astype(np.float64) - 127.0), 8, axis=1)[..., None]
    return vals.transpose(0, 1, 3, 2).reshape(g * 512, n)


def planes(y):
    n, m = y.shape
    v = y.astype(np.float32).astype(ml_dtypes.bfloat16).astype(np.float64).reshape(n // 32, 32, m)
    top = np.abs(v).max(1)
    byte = np.clip(np.where(top > 0, np.frexp(top)[1] - 1 + 127 - 7, 1), 1, 254)
    codes = (v * np.exp2(127.0 - byte)[:, None, :]).reshape(n, m).astype(np.float32).astype(ml_dtypes.float8_e4m3fn).view(np.uint8)
    words = codes.reshape(n // 512, 128, 4, m).transpose(0, 1, 3, 2)
    return np.ascontiguousarray(words), np.ascontiguousarray(byte.astype(np.uint8).reshape(n // 512, 16, m))


K, N, T, J = 512, 512, 2048, 1024


def setup_inputs():
    n = np.random.standard_normal
    s = mx_kscale(K)[:, None]
    p_tab = pack_weight(n((K, T)) * s, "e4m3")
    p_wk = pack_weight(n((K, N)) / np.sqrt(K) / s, "e4m3")
    p_wv4 = pack_weight(n((K, N)) / np.sqrt(K) / s, "e2m1")
    return {
        "tab_words": p_tab[0],
        "tab_scales": p_tab[1],
        "wk_words": p_wk[0],
        "wk_scales": p_wk[1],
        "wv4_words": p_wv4[0],
        "wv4_scales": p_wv4[1],
        "wvd": (0.4 * (n((K, N)) / np.sqrt(K) / s)).astype(np.float32),
        "st": (n((N, J))).astype(np.float32),
        "rT": (n((N, T))).astype(np.float32),
        "offs": striped(np.random.permutation(T)[:J]),
    }


def reference(tab_words, tab_scales, wk_words, wk_scales, wv4_words, wv4_scales, wvd, st, rT, offs):
    idx = unstriped(offs)
    tab_ = unpack_weight(tab_words, tab_scales, "e4m3")[:, idx]
    wk_ = unpack_weight(wk_words, wk_scales, "e4m3")
    wv4_ = unpack_weight(wv4_words, wv4_scales, "e2m1")
    wvd_ = mxq(f64(wvd), 0, "e4m3")
    ke = wk_.T @ tab_
    ve = wv4_.T @ tab_ + wvd_.T @ tab_
    gate = np.tanh(ke * f64(st))
    out_0 = f64(rT)[:, idx] + gate * ve
    return (out_0,) + planes(out_0)

@@ -1,0 +1,180 @@
+from contextlib import ExitStack
+
+import concourse.mybir as mybir
+
+K, N, T, J = 512, 512, 2048, 1024
+FLOPS = 3 * 2 * K * N * J
+
+F32 = mybir.dt.float32
+BF16 = mybir.dt.bfloat16
+I32 = mybir.dt.int32
+U32 = mybir.dt.uint32
+U16 = mybir.dt.uint16
+U8 = mybir.dt.uint8
+FP8X4 = mybir.dt.float8_e4m3fn_x4
+FP4X4 = mybir.dt.float4_e2m1fn_x4
+MULT = mybir.AluOpType.mult
+ADD = mybir.AluOpType.add
+TANH = mybir.ActivationFunctionType.Tanh
+
+P = 128
+PACK = 4
+BANK = 512
+HALVES = J // BANK
+WK_ROW = 4
+
+
+def tile_list_engram_dl_tanhLP_kernel(
+    tc, tab_words, tab_scales, wk_words, wk_scales, wv4_words, wv4_scales, wvd, st, rT, offs, out_0, out_1, out_2
+):
+    nc = tc.nc
+    with ExitStack() as ctx:
+        keep = ctx.enter_context(tc.tile_pool(name="keep", bufs=1))
+        ring = ctx.enter_context(tc.tile_pool(name="ring", bufs=3))
+        psum = ctx.enter_context(tc.psum_pool(name="psum", bufs=4))
+
+        offsets = keep.tile([P, J // 16], U16, name="offsets")
+        tab_w = keep.tile([P, T], U32, name="tab_w", align_bytes=64)
+        tab_s = keep.tile([P, T], U8, name="tab_s", align_bytes=64)
+        wk_raw = keep.tile([P, N], I32, name="wk_raw", align_bytes=64)
+        wv4_raw = keep.tile([P, 2 * N], U8, name="wv4_raw", align_bytes=64)
+        ws_raw = keep.tile([P, N], U8, name="ws_raw", align_bytes=64)
+        wvd_raw = keep.tile([P, PACK, N], F32, name="wvd_raw", align_bytes=64)
+        st_sb = [keep.tile([P, J], F32, name="st%d" % t, align_bytes=64) for t in range(PACK)]
+        r_sb = [keep.tile([P, T], F32, name="r%d" % t, align_bytes=64) for t in range(PACK)]
+
+        def load_scale_rows(engine, plane, first_row, scales):
+            for q in range(4):
+                rows = slice(32 * q + first_row, 32 * q + first_row + 4)
+                engine.dma_start(plane[rows, :].bitcast(I32), scales[0, 4 * q : 4 * q + 4, :].bitcast(I32))
+
+        nc.vector.memset(tab_s[:].bitcast(I32), 0)
+        nc.gpsimd.memset(ws_raw[:].bitcast(I32), 0)
+        st_rows = st.rearrange("(p t) j -> p t j", t=PACK)
+        r_rows = rT.rearrange("(p t) c -> p t c", t=PACK)
+        out_rows = out_0.rearrange("(p t) j -> p t j", t=PACK)
+
+        nc.sync.dma_start(offsets[:], offs)
+        nc.sync.dma_start(tab_w[:].bitcast(I32), tab_words[0].rearrange("p t i -> p (t i)").bitcast(I32))
+        load_scale_rows(nc.scalar, tab_s, 0, tab_scales)
+        load_scale_rows(nc.gpsimd, ws_raw, WK_ROW, wk_scales)
+        nc.sync.dma_start(wvd_raw[:], wvd.rearrange("(p i) n -> p i n", i=PACK))
+        nc.sync.dma_start(wk_raw[:], wk_words[0].rearrange("p n i -> p (n i)").bitcast(I32))
+        nc.sync.dma_start(wv4_raw[:].bitcast(I32), wv4_words[0].bitcast(I32))
+        load_scale_rows(nc.sync, ws_raw, 0, wv4_scales)
+        for t in range(PACK):
+            nc.sync.dma_start(st_sb[t][:], st_rows[:, t, :])
+            nc.sync.dma_start(r_sb[t][:], r_rows[:, t, :])
+
+        got_s = keep.tile([P, J], U8, name="got_s", align_bytes=64)
+        got_w = [keep.tile([P, BANK], U32, name="got_w%d" % h, align_bytes=64) for h in range(HALVES)]
+        wk_w = keep.tile([P, N], I32, name="wk_w", align_bytes=64)
+        wv4_w = keep.tile([P, 2 * N], U8, name="wv4_w", align_bytes=64)
+        w_s = keep.tile([P, N], U8, name="w_s", align_bytes=64)
+        wvd_bf = keep.tile([P, PACK * N], BF16, name="wvd_bf", align_bytes=64)
+        wvd_w = keep.tile([P, N], U32, name="wvd_w", align_bytes=64)
+        wvd_s = keep.tile([P, N], U8, name="wvd_s", align_bytes=64)
+
+        def listed(window, j0, j1):
+            return window[:].indirect(offsets[:, j0 // 16 : j1 // 16])
+
+        nc.vector.tensor_copy(got_s[:], listed(tab_s, 0, J))
+        nc.vector.tensor_copy(got_w[0][:], listed(tab_w, 0, BANK))
+        nc.vector.tensor_copy(
+            wk_w[:].rearrange("p (t m) -> p m t", t=PACK), wk_raw[:].rearrange("p (m t) -> p m t", t=PACK)
+        )
+        nc.vector.tensor_copy(
+            w_s[:].rearrange("p (t m) -> p t m", t=PACK), ws_raw[:].rearrange("p (m t) -> p t m", t=PACK)
+        )
+        nc.vector.tensor_copy(got_w[1][:], listed(tab_w, BANK, J))
+        nc.vector.tensor_copy(
+            wv4_w[:].rearrange("p (t m b) -> p t m b", t=PACK, b=2),
+            wv4_raw[:].rearrange("p (m t b) -> p t m b", t=PACK, b=2),
+        )
+        nc.scalar.copy(
+            wvd_bf[:].rearrange("p (t m i) -> p m t i", t=PACK, i=PACK),
+            wvd_raw[:].rearrange("p i (m t) -> p m t i", t=PACK),
+        )
+
+        y = [keep.tile([P, PACK, BANK], F32, name="y%d" % h, align_bytes=64) for h in range(HALVES)]
+        y_w = keep.tile([P, J], U32, name="y_w", align_bytes=64)
+        y_s = keep.tile([P, J], U8, name="y_s", align_bytes=64)
+        out_words = out_1[0].rearrange("p j i -> p (j i)").bitcast(I32)
+
+        units = [(0, 0), (0, 1), (1, 0), (1, 1), (2, 0), (3, 0), (2, 1), (3, 1)]
+        gates = {}
+        gated = {}
+
+        def key_side(u):
+            t, h = units[u]
+            m = slice(P * t, P * (t + 1))
+            cols = slice(BANK * h, BANK * (h + 1))
+            ke = psum.tile([P, BANK], F32, name="ke")
+            nc.tensor.matmul_mx(
+                ke[:], wk_w[:, m].bitcast(FP8X4), w_s[WK_ROW:P, m], got_w[h][:].bitcast(FP8X4), got_s[:, cols],
+                start=True, stop=True,
+            )
+            score = ring.tile([P, BANK], F32, name="score")
+            nc.vector.tensor_tensor(score[:], ke[:], st_sb[t][:, cols], MULT)
+            gate = ring.tile([P, BANK], F32, name="gate")
+            nc.scalar.activation(gate[:], score[:], TANH)
+            gates[u] = gate
+
+        def value_side(u):
+            t, h = units[u]
+            m = slice(P * t, P * (t + 1))
+            cols = slice(BANK * h, BANK * (h + 1))
+            ve = psum.tile([P, BANK], F32, name="ve")
+            moving = got_w[h][:].bitcast(FP8X4)
+            nc.tensor.matmul_mx(
+                ve[:], wv4_w[:, 2 * P * t : 2 * P * (t + 1)].bitcast(FP4X4), w_s[:, m], moving, got_s[:, cols],
+                start=True, stop=False,
+            )
+            nc.tensor.matmul_mx(
+                ve[:], wvd_w[:, m].bitcast(FP8X4), wvd_s[:, m], moving, got_s[:, cols], start=False, stop=True
+            )
+            product = ring.tile([P, BANK], F32, name="product")
+            nc.vector.tensor_tensor(product[:], ve[:], gates[u][:], MULT)
+            gated[u] = product
+
+        def add_record(u, c0, c1):
+            t, h = units[u]
+            j0, j1 = BANK * h + c0, BANK * h + c1
+            nc.vector.tensor_tensor(y[h][:, t, c0:c1], listed(r_sb[t], j0, j1), gated[u][:, c0:c1], ADD)
+            nc.sync.dma_start(out_rows[:, t, j0:j1], y[h][:, t, c0:c1])
+
+        def round_columns(copy, h, c0, c1):
+            rounded = keep.tile([P, PACK * (c1 - c0)], BF16, name="rounded%d_%d" % (h, c0), align_bytes=64)
+            copy(
+                rounded[:].rearrange("p (c i t) -> p c t i", i=4, t=PACK),
+                y[h][:, :, c0:c1].rearrange("p t (c i) -> p c t i", i=4),
+            )
+            return rounded
+
+        def quantise_columns(rounded, j0, j1):
+            nc.vector.quantize_mx(y_w[:, j0:j1].bitcast(FP8X4), y_s[:, j0:j1], rounded[:])
+            nc.sync.dma_start(out_words[:, j0:j1], y_w[:, j0:j1].bitcast(I32))
+
+        last = len(units) - 1
+        key_side(0)
+        key_side(1)
+        nc.vector.quantize_mx(wvd_w[:].bitcast(FP8X4), wvd_s[:], wvd_bf[:])
+        value_side(0)
+        for u in range(last):
+            if u + 2 <= last:
+                key_side(u + 2)
+            value_side(u + 1)
+            add_record(u, 0, BANK)
+            if units[u] == (PACK - 1, 0):
+                first_half = round_columns(nc.scalar.copy, 0, 0, BANK)
+        mid = BANK // 2
+        add_record(last, 0, mid)
+        third = round_columns(nc.scalar.copy, 1, 0, mid)
+        add_record(last, mid, BANK)
+        quantise_columns(first_half, 0, BANK)
+        fourth = round_columns(nc.vector.tensor_copy, 1, mid, BANK)
+        quantise_columns(third, BANK, BANK + mid)
+        quantise_columns(fourth, BANK + mid, J)
+        for q in range(4):
+            engine = nc.scalar if q < 2 else nc.sync
+            engine.dma_start(out_2[0, 4 * q : 4 * q + 4, :].bitcast(I32), y_s[32 * q : 32 * q + 4, :].bitcast(I32))

@@ -21,7 +21,6 @@ P = 128
 PACK = 4
 BANK = 512
 HALVES = J // BANK
-WK_ROW = 4
 
 
 def tile_list_engram_dl_tanhLP_kernel(
@@ -30,7 +29,7 @@ def tile_list_engram_dl_tanhLP_kernel(
     nc = tc.nc
     with ExitStack() as ctx:
         keep = ctx.enter_context(tc.tile_pool(name="keep", bufs=1))
-        ring = ctx.enter_context(tc.tile_pool(name="ring", bufs=3))
+        ring = ctx.enter_context(tc.tile_pool(name="ring", bufs=4))
         psum = ctx.enter_context(tc.psum_pool(name="psum", bufs=4))
 
         offsets = keep.tile([P, J // 16], U16, name="offsets")
@@ -38,39 +37,48 @@ def tile_list_engram_dl_tanhLP_kernel(
         tab_s = keep.tile([P, T], U8, name="tab_s", align_bytes=64)
         wk_raw = keep.tile([P, N], I32, name="wk_raw", align_bytes=64)
         wv4_raw = keep.tile([P, 2 * N], U8, name="wv4_raw", align_bytes=64)
-        ws_raw = keep.tile([P, N], U8, name="ws_raw", align_bytes=64)
-        wvd_raw = keep.tile([P, PACK, N], F32, name="wvd_raw", align_bytes=64)
+        wks_raw = keep.tile([P, N], U8, name="wks_raw", align_bytes=64)
+        wv4s_raw = keep.tile([P, N], U8, name="wv4s_raw", align_bytes=64)
+        wvd_raw = [keep.tile([P, PACK, N // 2], F32, name="wvd_raw%d" % c, align_bytes=64) for c in range(2)]
         st_sb = [keep.tile([P, J], F32, name="st%d" % t, align_bytes=64) for t in range(PACK)]
         r_sb = [keep.tile([P, T], F32, name="r%d" % t, align_bytes=64) for t in range(PACK)]
 
-        def load_scale_rows(engine, plane, first_row, scales):
-            for q in range(4):
-                rows = slice(32 * q + first_row, 32 * q + first_row + 4)
-                engine.dma_start(plane[rows, :].bitcast(I32), scales[0, 4 * q : 4 * q + 4, :].bitcast(I32))
+        def load_scale_rows(plane, scales, quadrants):
+            for q in quadrants:
+                rows = slice(32 * q, 32 * q + 4)
+                nc.sync.dma_start(plane[rows, :].bitcast(I32), scales[0, 4 * q : 4 * q + 4, :].bitcast(I32))
 
-        nc.vector.memset(tab_s[:].bitcast(I32), 0)
-        nc.gpsimd.memset(ws_raw[:].bitcast(I32), 0)
+        nc.vector.memset(tab_s[:, 0 : T // 2].bitcast(I32), 0)
+        nc.gpsimd.memset(tab_s[:, T // 2 : T].bitcast(I32), 0)
+        nc.vector.memset(wks_raw[:].bitcast(I32), 0)
+        nc.vector.memset(wv4s_raw[:].bitcast(I32), 0)
         st_rows = st.rearrange("(p t) j -> p t j", t=PACK)
         r_rows = rT.rearrange("(p t) c -> p t c", t=PACK)
         out_rows = out_0.rearrange("(p t) j -> p t j", t=PACK)
 
+        wvd_rows = wvd.rearrange("(p i) n -> p i n", i=PACK)
         nc.sync.dma_start(offsets[:], offs)
-        nc.sync.dma_start(tab_w[:].bitcast(I32), tab_words[0].rearrange("p t i -> p (t i)").bitcast(I32))
-        load_scale_rows(nc.scalar, tab_s, 0, tab_scales)
-        load_scale_rows(nc.gpsimd, ws_raw, WK_ROW, wk_scales)
-        nc.sync.dma_start(wvd_raw[:], wvd.rearrange("(p i) n -> p i n", i=PACK))
         nc.sync.dma_start(wk_raw[:], wk_words[0].rearrange("p n i -> p (n i)").bitcast(I32))
         nc.sync.dma_start(wv4_raw[:].bitcast(I32), wv4_words[0].bitcast(I32))
-        load_scale_rows(nc.sync, ws_raw, 0, wv4_scales)
+        load_scale_rows(tab_s, tab_scales, range(4))
+        nc.sync.dma_start(tab_w[:].bitcast(I32), tab_words[0].rearrange("p t i -> p (t i)").bitcast(I32))
+        for c in range(2):
+            nc.sync.dma_start(wvd_raw[c][:], wvd_rows[:, :, c * N // 2 : (c + 1) * N // 2])
+        load_scale_rows(wks_raw, wk_scales, range(4))
+        load_scale_rows(wv4s_raw, wv4_scales, range(1))
+        nc.sync.dma_start(st_sb[0][:], st_rows[:, 0, :])
+        load_scale_rows(wv4s_raw, wv4_scales, range(1, 4))
         for t in range(PACK):
-            nc.sync.dma_start(st_sb[t][:], st_rows[:, t, :])
+            if t + 1 < PACK:
+                nc.sync.dma_start(st_sb[t + 1][:], st_rows[:, t + 1, :])
             nc.sync.dma_start(r_sb[t][:], r_rows[:, t, :])
 
         got_s = keep.tile([P, J], U8, name="got_s", align_bytes=64)
         got_w = [keep.tile([P, BANK], U32, name="got_w%d" % h, align_bytes=64) for h in range(HALVES)]
         wk_w = keep.tile([P, N], I32, name="wk_w", align_bytes=64)
         wv4_w = keep.tile([P, 2 * N], U8, name="wv4_w", align_bytes=64)
-        w_s = keep.tile([P, N], U8, name="w_s", align_bytes=64)
+        wk_s = keep.tile([P, N], U8, name="wk_s", align_bytes=64)
+        wv4_s = keep.tile([P, N], U8, name="wv4_s", align_bytes=64)
         wvd_bf = keep.tile([P, PACK * N], BF16, name="wvd_bf", align_bytes=64)
         wvd_w = keep.tile([P, N], U32, name="wvd_w", align_bytes=64)
         wvd_s = keep.tile([P, N], U8, name="wvd_s", align_bytes=64)
@@ -78,23 +86,25 @@ def tile_list_engram_dl_tanhLP_kernel(
         def listed(window, j0, j1):
             return window[:].indirect(offsets[:, j0 // 16 : j1 // 16])
 
-        nc.vector.tensor_copy(got_s[:], listed(tab_s, 0, J))
-        nc.vector.tensor_copy(got_w[0][:], listed(tab_w, 0, BANK))
         nc.vector.tensor_copy(
             wk_w[:].rearrange("p (t m) -> p m t", t=PACK), wk_raw[:].rearrange("p (m t) -> p m t", t=PACK)
         )
         nc.vector.tensor_copy(
-            w_s[:].rearrange("p (t m) -> p t m", t=PACK), ws_raw[:].rearrange("p (m t) -> p t m", t=PACK)
-        )
-        nc.vector.tensor_copy(got_w[1][:], listed(tab_w, BANK, J))
-        nc.vector.tensor_copy(
             wv4_w[:].rearrange("p (t m b) -> p t m b", t=PACK, b=2),
             wv4_raw[:].rearrange("p (m t b) -> p t m b", t=PACK, b=2),
         )
-        nc.scalar.copy(
-            wvd_bf[:].rearrange("p (t m i) -> p m t i", t=PACK, i=PACK),
-            wvd_raw[:].rearrange("p i (m t) -> p m t i", t=PACK),
-        )
+        nc.vector.tensor_copy(got_s[:], listed(tab_s, 0, J))
+        nc.vector.tensor_copy(got_w[0][:], listed(tab_w, 0, BANK))
+        nc.vector.tensor_copy(got_w[1][:], listed(tab_w, BANK, J))
+        for dealt, raw in ((wk_s, wks_raw), (wv4_s, wv4s_raw)):
+            nc.vector.tensor_copy(
+                dealt[:].rearrange("p (t m) -> p t m", t=PACK), raw[:].rearrange("p (m t) -> p t m", t=PACK)
+            )
+        for c in range(2):
+            nc.scalar.copy(
+                wvd_bf[:].rearrange("p (t m i) -> p m t i", t=PACK, i=PACK)[:, c * P // 2 : (c + 1) * P // 2],
+                wvd_raw[c][:].rearrange("p i (m t) -> p m t i", t=PACK),
+            )
 
         y = [keep.tile([P, PACK, BANK], F32, name="y%d" % h, align_bytes=64) for h in range(HALVES)]
         y_w = keep.tile([P, J], U32, name="y_w", align_bytes=64)
@@ -111,7 +121,7 @@ def tile_list_engram_dl_tanhLP_kernel(
             cols = slice(BANK * h, BANK * (h + 1))
             ke = psum.tile([P, BANK], F32, name="ke")
             nc.tensor.matmul_mx(
-                ke[:], wk_w[:, m].bitcast(FP8X4), w_s[WK_ROW:P, m], got_w[h][:].bitcast(FP8X4), got_s[:, cols],
+                ke[:], wk_w[:, m].bitcast(FP8X4), wk_s[:, m], got_w[h][:].bitcast(FP8X4), got_s[:, cols],
                 start=True, stop=True,
             )
             score = ring.tile([P, BANK], F32, name="score")
@@ -127,7 +137,7 @@ def tile_list_engram_dl_tanhLP_kernel(
             ve = psum.tile([P, BANK], F32, name="ve")
             moving = got_w[h][:].bitcast(FP8X4)
             nc.tensor.matmul_mx(
-                ve[:], wv4_w[:, 2 * P * t : 2 * P * (t + 1)].bitcast(FP4X4), w_s[:, m], moving, got_s[:, cols],
+                ve[:], wv4_w[:, 2 * P * t : 2 * P * (t + 1)].bitcast(FP4X4), wv4_s[:, m], moving, got_s[:, cols],
                 start=True, stop=False,
             )
             nc.tensor.matmul_mx(
@@ -157,8 +167,8 @@ def tile_list_engram_dl_tanhLP_kernel(
 
         last = len(units) - 1
         key_side(0)
-        key_side(1)
         nc.vector.quantize_mx(wvd_w[:].bitcast(FP8X4), wvd_s[:], wvd_bf[:])
+        key_side(1)
         value_side(0)
         for u in range(last):
             if u + 2 <= last:

@@ -41,10 +41,10 @@ def tile_list_engram_dl_tanhLP_kernel(
         wv4s_raw = keep.tile([P, N], U8, name="wv4s_raw", align_bytes=64)
         wvd_raw = [keep.tile([P, PACK, N // 2], F32, name="wvd_raw%d" % c, align_bytes=64) for c in range(2)]
         st_sb = [keep.tile([P, J], F32, name="st%d" % t, align_bytes=64) for t in range(PACK)]
-        r_sb = [keep.tile([P, T], F32, name="r%d" % t, align_bytes=64) for t in range(PACK)]
+        r_sb = [keep.tile([P, T], F32, name="r%d" % t, tag="plane%d" % t, align_bytes=64) for t in range(PACK)]
 
-        def load_scale_rows(plane, scales, quadrants):
-            for q in quadrants:
+        def load_scale_rows(plane, scales):
+            for q in range(4):
                 rows = slice(32 * q, 32 * q + 4)
                 nc.sync.dma_start(plane[rows, :].bitcast(I32), scales[0, 4 * q : 4 * q + 4, :].bitcast(I32))
 
@@ -60,17 +60,18 @@ def tile_list_engram_dl_tanhLP_kernel(
         nc.sync.dma_start(offsets[:], offs)
         nc.sync.dma_start(wk_raw[:], wk_words[0].rearrange("p n i -> p (n i)").bitcast(I32))
         nc.sync.dma_start(wv4_raw[:].bitcast(I32), wv4_words[0].bitcast(I32))
-        load_scale_rows(tab_s, tab_scales, range(4))
+        load_scale_rows(tab_s, tab_scales)
         nc.sync.dma_start(tab_w[:].bitcast(I32), tab_words[0].rearrange("p t i -> p (t i)").bitcast(I32))
         for c in range(2):
             nc.sync.dma_start(wvd_raw[c][:], wvd_rows[:, :, c * N // 2 : (c + 1) * N // 2])
-        load_scale_rows(wks_raw, wk_scales, range(4))
-        load_scale_rows(wv4s_raw, wv4_scales, range(1))
-        nc.sync.dma_start(st_sb[0][:], st_rows[:, 0, :])
-        load_scale_rows(wv4s_raw, wv4_scales, range(1, 4))
-        for t in range(PACK):
-            if t + 1 < PACK:
-                nc.sync.dma_start(st_sb[t + 1][:], st_rows[:, t + 1, :])
+        load_scale_rows(wks_raw, wk_scales)
+        for t in range(2):
+            nc.sync.dma_start(st_sb[t][:], st_rows[:, t, :])
+        load_scale_rows(wv4s_raw, wv4_scales)
+        nc.sync.dma_start(r_sb[0][:], r_rows[:, 0, :])
+        for t in range(2, PACK):
+            nc.sync.dma_start(st_sb[t][:], st_rows[:, t, :])
+        for t in range(1, PACK):
             nc.sync.dma_start(r_sb[t][:], r_rows[:, t, :])
 
         got_s = keep.tile([P, J], U8, name="got_s", align_bytes=64)
@@ -86,6 +87,11 @@ def tile_list_engram_dl_tanhLP_kernel(
         def listed(window, j0, j1):
             return window[:].indirect(offsets[:, j0 // 16 : j1 // 16])
 
+        def deal_scale_bytes(dealt, raw):
+            nc.vector.tensor_copy(
+                dealt[:].rearrange("p (t m) -> p t m", t=PACK), raw[:].rearrange("p (m t) -> p t m", t=PACK)
+            )
+
         nc.vector.tensor_copy(
             wk_w[:].rearrange("p (t m) -> p m t", t=PACK), wk_raw[:].rearrange("p (m t) -> p m t", t=PACK)
         )
@@ -96,10 +102,7 @@ def tile_list_engram_dl_tanhLP_kernel(
         nc.vector.tensor_copy(got_s[:], listed(tab_s, 0, J))
         nc.vector.tensor_copy(got_w[0][:], listed(tab_w, 0, BANK))
         nc.vector.tensor_copy(got_w[1][:], listed(tab_w, BANK, J))
-        for dealt, raw in ((wk_s, wks_raw), (wv4_s, wv4s_raw)):
-            nc.vector.tensor_copy(
-                dealt[:].rearrange("p (t m) -> p t m", t=PACK), raw[:].rearrange("p (m t) -> p t m", t=PACK)
-            )
+        deal_scale_bytes(wk_s, wks_raw)
         for c in range(2):
             nc.scalar.copy(
                 wvd_bf[:].rearrange("p (t m i) -> p m t i", t=PACK, i=PACK)[:, c * P // 2 : (c + 1) * P // 2],
@@ -115,7 +118,7 @@ def tile_list_engram_dl_tanhLP_kernel(
         gates = {}
         gated = {}
 
-        def key_side(u):
+        def key_side(u, score):
             t, h = units[u]
             m = slice(P * t, P * (t + 1))
             cols = slice(BANK * h, BANK * (h + 1))
@@ -124,13 +127,12 @@ def tile_list_engram_dl_tanhLP_kernel(
                 ke[:], wk_w[:, m].bitcast(FP8X4), wk_s[:, m], got_w[h][:].bitcast(FP8X4), got_s[:, cols],
                 start=True, stop=True,
             )
-            score = ring.tile([P, BANK], F32, name="score")
-            nc.vector.tensor_tensor(score[:], ke[:], st_sb[t][:, cols], MULT)
+            nc.vector.tensor_tensor(score, ke[:], st_sb[t][:, cols], MULT)
             gate = ring.tile([P, BANK], F32, name="gate")
-            nc.scalar.activation(gate[:], score[:], TANH)
+            nc.scalar.activation(gate[:], score, TANH)
             gates[u] = gate
 
-        def value_side(u):
+        def value_side(u, product, on_gpsimd=False):
             t, h = units[u]
             m = slice(P * t, P * (t + 1))
             cols = slice(BANK * h, BANK * (h + 1))
@@ -143,8 +145,12 @@ def tile_list_engram_dl_tanhLP_kernel(
             nc.tensor.matmul_mx(
                 ve[:], wvd_w[:, m].bitcast(FP8X4), wvd_s[:, m], moving, got_s[:, cols], start=False, stop=True
             )
-            product = ring.tile([P, BANK], F32, name="product")
-            nc.vector.tensor_tensor(product[:], ve[:], gates[u][:], MULT)
+            if on_gpsimd:
+                ve_sb = ring.tile([P, BANK], F32, name="ve_sb")
+                nc.scalar.copy(ve_sb[:], ve[:])
+                nc.gpsimd.tensor_tensor(product, ve_sb[:], gates[u][:], MULT)
+            else:
+                nc.vector.tensor_tensor(product, ve[:], gates[u][:], MULT)
             gated[u] = product
 
         def add_record(u, c0, c1):
@@ -166,16 +172,25 @@ def tile_list_engram_dl_tanhLP_kernel(
             nc.sync.dma_start(out_words[:, j0:j1], y_w[:, j0:j1].bitcast(I32))
 
         last = len(units) - 1
-        key_side(0)
+        scores = keep.tile([P, 4 * BANK], F32, name="scores")
+        key_side(0, scores[:, 0:BANK])
         nc.vector.quantize_mx(wvd_w[:].bitcast(FP8X4), wvd_s[:], wvd_bf[:])
-        key_side(1)
-        value_side(0)
-        for u in range(last):
-            if u + 2 <= last:
-                key_side(u + 2)
-            value_side(u + 1)
-            add_record(u, 0, BANK)
-            if units[u] == (PACK - 1, 0):
+        deal_scale_bytes(wv4_s, wv4s_raw)
+        for u in range(1, 4):
+            key_side(u, scores[:, u * BANK : (u + 1) * BANK])
+        for pair, work_tag in enumerate(("first_work", "plane0", "plane1", "plane1")):
+            even, odd = 2 * pair, 2 * pair + 1
+            work = keep.tile([P, 4 * BANK], F32, name="work%d" % pair, tag=work_tag, align_bytes=64)
+            value_side(even, work[:, 0:BANK])
+            inner = 0 < even < last - 1
+            if inner:
+                key_side(even + 2, work[:, 2 * BANK : 3 * BANK])
+                key_side(odd + 2, work[:, 3 * BANK : 4 * BANK])
+            value_side(odd, work[:, BANK : 2 * BANK], on_gpsimd=inner)
+            add_record(even, 0, BANK)
+            if odd < last:
+                add_record(odd, 0, BANK)
+            if units[odd] == (PACK - 1, 0):
                 first_half = round_columns(nc.scalar.copy, 0, 0, BANK)
         mid = BANK // 2
         add_record(last, 0, mid)

@@ -38,10 +38,10 @@ def tile_list_engram_dl_tanhLP_kernel(
         wk_raw = keep.tile([P, N], I32, name="wk_raw", align_bytes=64)
         wv4_raw = keep.tile([P, 2 * N], U8, name="wv4_raw", align_bytes=64)
         wks_raw = keep.tile([P, N], U8, name="wks_raw", align_bytes=64)
-        wv4s_raw = keep.tile([P, N], U8, name="wv4s_raw", align_bytes=64)
+        wv4s_raw = keep.tile([P, N], U8, name="wv4s_raw", tag="wv4s_then_scores", align_bytes=64)
         wvd_raw = [keep.tile([P, PACK, N // 2], F32, name="wvd_raw%d" % c, align_bytes=64) for c in range(2)]
         st_sb = [keep.tile([P, J], F32, name="st%d" % t, align_bytes=64) for t in range(PACK)]
-        r_sb = [keep.tile([P, T], F32, name="r%d" % t, tag="plane%d" % t, align_bytes=64) for t in range(PACK)]
+        r_sb = [keep.tile([P, T], F32, name="r%d" % t, align_bytes=64) for t in range(PACK)]
 
         def load_scale_rows(plane, scales):
             for q in range(4):
@@ -80,7 +80,7 @@ def tile_list_engram_dl_tanhLP_kernel(
         wv4_w = keep.tile([P, 2 * N], U8, name="wv4_w", align_bytes=64)
         wk_s = keep.tile([P, N], U8, name="wk_s", align_bytes=64)
         wv4_s = keep.tile([P, N], U8, name="wv4_s", align_bytes=64)
-        wvd_bf = keep.tile([P, PACK * N], BF16, name="wvd_bf", align_bytes=64)
+        wvd_bf = keep.tile([P, PACK * N], BF16, name="wvd_bf", tag="wvd_then_score", align_bytes=64)
         wvd_w = keep.tile([P, N], U32, name="wvd_w", align_bytes=64)
         wvd_s = keep.tile([P, N], U8, name="wvd_s", align_bytes=64)
 
@@ -118,7 +118,15 @@ def tile_list_engram_dl_tanhLP_kernel(
         gates = {}
         gated = {}
 
-        def key_side(u, score):
+        def times_psum(out, bank, other, on_gpsimd):
+            if on_gpsimd:
+                staged = ring.tile([P, BANK], F32, name="staged")
+                nc.scalar.copy(staged[:], bank[:])
+                nc.gpsimd.tensor_tensor(out, staged[:], other, MULT)
+            else:
+                nc.vector.tensor_tensor(out, bank[:], other, MULT)
+
+        def key_side(u, score, on_gpsimd=False):
             t, h = units[u]
             m = slice(P * t, P * (t + 1))
             cols = slice(BANK * h, BANK * (h + 1))
@@ -127,7 +135,7 @@ def tile_list_engram_dl_tanhLP_kernel(
                 ke[:], wk_w[:, m].bitcast(FP8X4), wk_s[:, m], got_w[h][:].bitcast(FP8X4), got_s[:, cols],
                 start=True, stop=True,
             )
-            nc.vector.tensor_tensor(score, ke[:], st_sb[t][:, cols], MULT)
+            times_psum(score, ke, st_sb[t][:, cols], on_gpsimd)
             gate = ring.tile([P, BANK], F32, name="gate")
             nc.scalar.activation(gate[:], score, TANH)
             gates[u] = gate
@@ -145,12 +153,7 @@ def tile_list_engram_dl_tanhLP_kernel(
             nc.tensor.matmul_mx(
                 ve[:], wvd_w[:, m].bitcast(FP8X4), wvd_s[:, m], moving, got_s[:, cols], start=False, stop=True
             )
-            if on_gpsimd:
-                ve_sb = ring.tile([P, BANK], F32, name="ve_sb")
-                nc.scalar.copy(ve_sb[:], ve[:])
-                nc.gpsimd.tensor_tensor(product, ve_sb[:], gates[u][:], MULT)
-            else:
-                nc.vector.tensor_tensor(product, ve[:], gates[u][:], MULT)
+            times_psum(product, ve, gates[u][:], on_gpsimd)
             gated[u] = product
 
         def add_record(u, c0, c1):
@@ -172,21 +175,26 @@ def tile_list_engram_dl_tanhLP_kernel(
             nc.sync.dma_start(out_words[:, j0:j1], y_w[:, j0:j1].bitcast(I32))
 
         last = len(units) - 1
-        scores = keep.tile([P, 4 * BANK], F32, name="scores")
-        key_side(0, scores[:, 0:BANK])
         nc.vector.quantize_mx(wvd_w[:].bitcast(FP8X4), wvd_s[:], wvd_bf[:])
+        first_score = keep.tile([P, BANK], F32, name="first_score", tag="wvd_then_score", align_bytes=64)
+        key_side(0, first_score[:])
         deal_scale_bytes(wv4_s, wv4s_raw)
+        scores = keep.tile([P, 3 * BANK], F32, name="scores", tag="wv4s_then_scores", align_bytes=64)
         for u in range(1, 4):
-            key_side(u, scores[:, u * BANK : (u + 1) * BANK])
-        for pair, work_tag in enumerate(("first_work", "plane0", "plane1", "plane1")):
-            even, odd = 2 * pair, 2 * pair + 1
-            work = keep.tile([P, 4 * BANK], F32, name="work%d" % pair, tag=work_tag, align_bytes=64)
-            value_side(even, work[:, 0:BANK])
+            key_side(u, scores[:, (u - 1) * BANK : u * BANK], on_gpsimd=u == 3)
+        for even in range(0, len(units), 2):
+            odd = even + 1
+            odd_work = keep.tile([P, 2 * BANK], F32, name="odd_work")
+            if odd == last:
+                value_side(even, odd_work[:, BANK : 2 * BANK])
+            else:
+                even_work = keep.tile([P, 3 * BANK], F32, name="even_work")
+                value_side(even, even_work[:, 0:BANK])
             inner = 0 < even < last - 1
             if inner:
-                key_side(even + 2, work[:, 2 * BANK : 3 * BANK])
-                key_side(odd + 2, work[:, 3 * BANK : 4 * BANK])
-            value_side(odd, work[:, BANK : 2 * BANK], on_gpsimd=inner)
+                key_side(even + 2, even_work[:, BANK : 2 * BANK])
+                key_side(odd + 2, even_work[:, 2 * BANK : 3 * BANK])
+            value_side(odd, odd_work[:, 0:BANK], on_gpsimd=inner)
             add_record(even, 0, BANK)
             if odd < last:
                 add_record(odd, 0, BANK)

from contextlib import ExitStack

import concourse.mybir as mybir

K, N, T, J = 512, 512, 2048, 1024
FLOPS = 3 * 2 * K * N * J

F32 = mybir.dt.float32
BF16 = mybir.dt.bfloat16
I32 = mybir.dt.int32
U32 = mybir.dt.uint32
U16 = mybir.dt.uint16
U8 = mybir.dt.uint8
FP8X4 = mybir.dt.float8_e4m3fn_x4
FP4X4 = mybir.dt.float4_e2m1fn_x4
MULT = mybir.AluOpType.mult
ADD = mybir.AluOpType.add
TANH = mybir.ActivationFunctionType.Tanh

P = 128
PACK = 4
BANK = 512
HALVES = J // BANK


def tile_list_engram_dl_tanhLP_kernel(
    tc, tab_words, tab_scales, wk_words, wk_scales, wv4_words, wv4_scales, wvd, st, rT, offs, out_0, out_1, out_2
):
    nc = tc.nc
    with ExitStack() as ctx:
        keep = ctx.enter_context(tc.tile_pool(name="keep", bufs=1))
        ring = ctx.enter_context(tc.tile_pool(name="ring", bufs=4))
        psum = ctx.enter_context(tc.psum_pool(name="psum", bufs=4))

        offsets = keep.tile([P, J // 16], U16, name="offsets")
        tab_w = keep.tile([P, T], U32, name="tab_w", align_bytes=64)
        tab_s = keep.tile([P, T], U8, name="tab_s", align_bytes=64)
        wk_raw = keep.tile([P, N], I32, name="wk_raw", align_bytes=64)
        wv4_raw = keep.tile([P, 2 * N], U8, name="wv4_raw", align_bytes=64)
        wks_raw = keep.tile([P, N], U8, name="wks_raw", align_bytes=64)
        wv4s_raw = keep.tile([P, N], U8, name="wv4s_raw", tag="wv4s_then_scores", align_bytes=64)
        wvd_raw = [keep.tile([P, PACK, N // 2], F32, name="wvd_raw%d" % c, align_bytes=64) for c in range(2)]
        st_sb = [keep.tile([P, J], F32, name="st%d" % t, align_bytes=64) for t in range(PACK)]
        r_sb = [keep.tile([P, T], F32, name="r%d" % t, align_bytes=64) for t in range(PACK)]

        def load_scale_rows(plane, scales):
            for q in range(4):
                rows = slice(32 * q, 32 * q + 4)
                nc.sync.dma_start(plane[rows, :].bitcast(I32), scales[0, 4 * q : 4 * q + 4, :].bitcast(I32))

        nc.vector.memset(tab_s[:, 0 : T // 2].bitcast(I32), 0)
        nc.gpsimd.memset(tab_s[:, T // 2 : T].bitcast(I32), 0)
        nc.vector.memset(wks_raw[:].bitcast(I32), 0)
        nc.vector.memset(wv4s_raw[:].bitcast(I32), 0)
        st_rows = st.rearrange("(p t) j -> p t j", t=PACK)
        r_rows = rT.rearrange("(p t) c -> p t c", t=PACK)
        out_rows = out_0.rearrange("(p t) j -> p t j", t=PACK)

        wvd_rows = wvd.rearrange("(p i) n -> p i n", i=PACK)
        nc.sync.dma_start(offsets[:], offs)
        nc.sync.dma_start(wk_raw[:], wk_words[0].rearrange("p n i -> p (n i)").bitcast(I32))
        nc.sync.dma_start(wv4_raw[:].bitcast(I32), wv4_words[0].bitcast(I32))
        load_scale_rows(tab_s, tab_scales)
        nc.sync.dma_start(tab_w[:].bitcast(I32), tab_words[0].rearrange("p t i -> p (t i)").bitcast(I32))
        for c in range(2):
            nc.sync.dma_start(wvd_raw[c][:], wvd_rows[:, :, c * N // 2 : (c + 1) * N // 2])
        load_scale_rows(wks_raw, wk_scales)
        for t in range(2):
            nc.sync.dma_start(st_sb[t][:], st_rows[:, t, :])
        load_scale_rows(wv4s_raw, wv4_scales)
        nc.sync.dma_start(r_sb[0][:], r_rows[:, 0, :])
        for t in range(2, PACK):
            nc.sync.dma_start(st_sb[t][:], st_rows[:, t, :])
        for t in range(1, PACK):
            nc.sync.dma_start(r_sb[t][:], r_rows[:, t, :])

        got_s = keep.tile([P, J], U8, name="got_s", align_bytes=64)
        got_w = [keep.tile([P, BANK], U32, name="got_w%d" % h, align_bytes=64) for h in range(HALVES)]
        wk_w = keep.tile([P, N], I32, name="wk_w", align_bytes=64)
        wv4_w = keep.tile([P, 2 * N], U8, name="wv4_w", align_bytes=64)
        wk_s = keep.tile([P, N], U8, name="wk_s", align_bytes=64)
        wv4_s = keep.tile([P, N], U8, name="wv4_s", align_bytes=64)
        wvd_bf = keep.tile([P, PACK * N], BF16, name="wvd_bf", tag="wvd_then_score", align_bytes=64)
        wvd_w = keep.tile([P, N], U32, name="wvd_w", align_bytes=64)
        wvd_s = keep.tile([P, N], U8, name="wvd_s", align_bytes=64)

        def listed(window, j0, j1):
            return window[:].indirect(offsets[:, j0 // 16 : j1 // 16])

        def deal_scale_bytes(dealt, raw):
            nc.vector.tensor_copy(
                dealt[:].rearrange("p (t m) -> p t m", t=PACK), raw[:].rearrange("p (m t) -> p t m", t=PACK)
            )

        nc.vector.tensor_copy(
            wk_w[:].rearrange("p (t m) -> p m t", t=PACK), wk_raw[:].rearrange("p (m t) -> p m t", t=PACK)
        )
        nc.vector.tensor_copy(
            wv4_w[:].rearrange("p (t m b) -> p t m b", t=PACK, b=2),
            wv4_raw[:].rearrange("p (m t b) -> p t m b", t=PACK, b=2),
        )
        nc.vector.tensor_copy(got_s[:], listed(tab_s, 0, J))
        nc.vector.tensor_copy(got_w[0][:], listed(tab_w, 0, BANK))
        nc.vector.tensor_copy(got_w[1][:], listed(tab_w, BANK, J))
        deal_scale_bytes(wk_s, wks_raw)
        for c in range(2):
            nc.scalar.copy(
                wvd_bf[:].rearrange("p (t m i) -> p m t i", t=PACK, i=PACK)[:, c * P // 2 : (c + 1) * P // 2],
                wvd_raw[c][:].rearrange("p i (m t) -> p m t i", t=PACK),
            )

        y = [keep.tile([P, PACK, BANK], F32, name="y%d" % h, align_bytes=64) for h in range(HALVES)]
        y_w = keep.tile([P, J], U32, name="y_w", align_bytes=64)
        y_s = keep.tile([P, J], U8, name="y_s", align_bytes=64)
        out_words = out_1[0].rearrange("p j i -> p (j i)").bitcast(I32)

        units = [(0, 0), (0, 1), (1, 0), (1, 1), (2, 0), (3, 0), (2, 1), (3, 1)]
        gates = {}
        gated = {}

        def times_psum(out, bank, other, on_gpsimd):
            if on_gpsimd:
                staged = ring.tile([P, BANK], F32, name="staged")
                nc.scalar.copy(staged[:], bank[:])
                nc.gpsimd.tensor_tensor(out, staged[:], other, MULT)
            else:
                nc.vector.tensor_tensor(out, bank[:], other, MULT)

        def key_side(u, score, on_gpsimd=False):
            t, h = units[u]
            m = slice(P * t, P * (t + 1))
            cols = slice(BANK * h, BANK * (h + 1))
            ke = psum.tile([P, BANK], F32, name="ke")
            nc.tensor.matmul_mx(
                ke[:], wk_w[:, m].bitcast(FP8X4), wk_s[:, m], got_w[h][:].bitcast(FP8X4), got_s[:, cols],
                start=True, stop=True,
            )
            times_psum(score, ke, st_sb[t][:, cols], on_gpsimd)
            gate = ring.tile([P, BANK], F32, name="gate")
            nc.scalar.activation(gate[:], score, TANH)
            gates[u] = gate

        def value_side(u, product, on_gpsimd=False):
            t, h = units[u]
            m = slice(P * t, P * (t + 1))
            cols = slice(BANK * h, BANK * (h + 1))
            ve = psum.tile([P, BANK], F32, name="ve")
            moving = got_w[h][:].bitcast(FP8X4)
            nc.tensor.matmul_mx(
                ve[:], wv4_w[:, 2 * P * t : 2 * P * (t + 1)].bitcast(FP4X4), wv4_s[:, m], moving, got_s[:, cols],
                start=True, stop=False,
            )
            nc.tensor.matmul_mx(
                ve[:], wvd_w[:, m].bitcast(FP8X4), wvd_s[:, m], moving, got_s[:, cols], start=False, stop=True
            )
            times_psum(product, ve, gates[u][:], on_gpsimd)
            gated[u] = product

        def add_record(u, c0, c1):
            t, h = units[u]
            j0, j1 = BANK * h + c0, BANK * h + c1
            nc.vector.tensor_tensor(y[h][:, t, c0:c1], listed(r_sb[t], j0, j1), gated[u][:, c0:c1], ADD)
            nc.sync.dma_start(out_rows[:, t, j0:j1], y[h][:, t, c0:c1])

        def round_columns(copy, h, c0, c1):
            rounded = keep.tile([P, PACK * (c1 - c0)], BF16, name="rounded%d_%d" % (h, c0), align_bytes=64)
            copy(
                rounded[:].rearrange("p (c i t) -> p c t i", i=4, t=PACK),
                y[h][:, :, c0:c1].rearrange("p t (c i) -> p c t i", i=4),
            )
            return rounded

        def quantise_columns(rounded, j0, j1):
            nc.vector.quantize_mx(y_w[:, j0:j1].bitcast(FP8X4), y_s[:, j0:j1], rounded[:])
            nc.sync.dma_start(out_words[:, j0:j1], y_w[:, j0:j1].bitcast(I32))

        last = len(units) - 1
        nc.vector.quantize_mx(wvd_w[:].bitcast(FP8X4), wvd_s[:], wvd_bf[:])
        first_score = keep.tile([P, BANK], F32, name="first_score", tag="wvd_then_score", align_bytes=64)
        key_side(0, first_score[:])
        deal_scale_bytes(wv4_s, wv4s_raw)
        scores = keep.tile([P, 3 * BANK], F32, name="scores", tag="wv4s_then_scores", align_bytes=64)
        for u in range(1, 4):
            key_side(u, scores[:, (u - 1) * BANK : u * BANK], on_gpsimd=u == 3)
        for even in range(0, len(units), 2):
            odd = even + 1
            odd_work = keep.tile([P, 2 * BANK], F32, name="odd_work")
            if odd == last:
                value_side(even, odd_work[:, BANK : 2 * BANK])
            else:
                even_work = keep.tile([P, 3 * BANK], F32, name="even_work")
                value_side(even, even_work[:, 0:BANK])
            inner = 0 < even < last - 1
            if inner:
                key_side(even + 2, even_work[:, BANK : 2 * BANK])
                key_side(odd + 2, even_work[:, 2 * BANK : 3 * BANK])
            value_side(odd, odd_work[:, 0:BANK], on_gpsimd=inner)
            add_record(even, 0, BANK)
            if odd < last:
                add_record(odd, 0, BANK)
            if units[odd] == (PACK - 1, 0):
                first_half = round_columns(nc.scalar.copy, 0, 0, BANK)
        mid = BANK // 2
        add_record(last, 0, mid)
        third = round_columns(nc.scalar.copy, 1, 0, mid)
        add_record(last, mid, BANK)
        quantise_columns(first_half, 0, BANK)
        fourth = round_columns(nc.vector.tensor_copy, 1, mid, BANK)
        quantise_columns(third, BANK, BANK + mid)
        quantise_columns(fourth, BANK + mid, J)
        for q in range(4):
            engine = nc.scalar if q < 2 else nc.sync
            engine.dma_start(out_2[0, 4 * q : 4 * q + 4, :].bitcast(I32), y_s[32 * q : 32 * q + 4, :].bitcast(I32))
